import numpy as np
import ml_dtypes


def mxq(x, axis, fmt="e4m3"):
    dtype, down = {"e4m3": (ml_dtypes.float8_e4m3fn, 7), "e5m2": (ml_dtypes.float8_e5m2, 14)}[fmt]
    v = np.moveaxis(np.asarray(x, np.float32).astype(ml_dtypes.bfloat16).astype(np.float64), axis, -1)
    blocks = v.reshape(v.shape[:-1] + (-1, 32))
    amax = np.abs(blocks).max(-1, keepdims=True)
    byte = np.maximum(np.where(amax > 0, np.frexp(amax)[1] - 1 + 127, 0) - down, 1)
    scale = np.exp2(byte - 127.0)
    codes = (blocks / scale).astype(np.float32).astype(dtype).astype(np.float64)
    return np.moveaxis((codes * scale).reshape(v.shape), -1, axis)


WIDE = False


def mx_kscale(k):
    if not WIDE:
        return np.ones(k)
    levels = np.array([30, -30])
    if k % 512:
        return np.exp2(np.random.permutation(np.resize(levels, k // 32))).repeat(32)
    a = np.empty((k // 512, 16))
    for p in range(k // 512):
        a[p, :8] = np.random.permutation(np.resize(levels, 8))
        for g in range(8):
            far = levels[np.abs(levels - a[p, g]) >= 10]
            a[p, g + 8] = far[np.random.randint(len(far))]
    return np.exp2(a.ravel()).repeat(32)


def f64(x):
    return np.asarray(x).astype(np.float64)


def striped(idx):
    return np.tile(np.asarray(idx).reshape(-1, 16).T, (8, 1)).astype(np.uint16)


def unstriped(offs):
    return offs[:16].T.reshape(-1).astype(np.int64)


def striped8(idx):
    return np.asarray(idx).reshape(8, -1, 16).transpose(0, 2, 1).reshape(128, -1).astype(np.uint16)


def unstriped8(offs):
    return offs.reshape(8, 16, -1).transpose(0, 2, 1).reshape(8, -1).astype(np.int64)


def pick8(x, idx, run):
    r = np.arange(len(x))
    return x[r[:, None], idx[r % (8 * run) // run]]


E2M1 = np.array([0.0, 0.5, 1.0, 1.5, 2.0, 3.0, 4.0, 6.0, -0.0, -0.5, -1.0, -1.5, -2.0, -3.0, -4.0, -6.0])


def pack_weight(w, fmt):
    k, n = w.shape
    w = f64(np.asarray(w, np.float32).astype(ml_dtypes.bfloat16)).reshape(k // 32, 32, n)
    amax = np.abs(w).max(1)
    if fmt == "e4m3":
        byte = np.frexp(amax)[1] - 1 + 127 - 7
    else:
        mant, ex = np.frexp(amax / 6.0)
        byte = np.where(mant > 0.5, ex, ex - 1) + 127
    byte = np.clip(np.where(amax > 0, byte, 1), 1, 254)
    scaled = (w * np.exp2(127.0 - byte)[:, None, :]).reshape(k, n).astype(np.float32)
    by_word = np.ascontiguousarray(scaled.reshape(k // 512, 128, 4, n).transpose(0, 1, 3, 2))
    if fmt == "e4m3":
        words = by_word.astype(ml_dtypes.float8_e4m3fn).view(np.uint8)
    else:
        c = by_word.astype(ml_dtypes.float4_e2m1fn).view(np.uint8) & 0xF
        words = (c[..., 0::2] | (c[..., 1::2] << 4)).reshape(k // 512, 128, 2 * n)
    return np.ascontiguousarray(words), np.ascontiguousarray(byte.astype(np.uint8).reshape(k // 512, 16, n))


def unpack_weight(words, scales, fmt):
    g, _, n = scales.shape
    words = np.ascontiguousarray(words).reshape(g, 128, n, -1)
    if fmt == "e4m3":
        vals = words.view(ml_dtypes.float8_e4m3fn).astype(np.float64)
    else:
        nib = np.empty((g, 128, n, 4), np.uint8)
        nib[..., 0::2] = words & 0xF
        nib[..., 1::2] = words >> 4
        vals = E2M1[nib]
    vals = vals * np.repeat(np.exp2(scales.astype(np.float64) - 127.0), 8, axis=1)[..., None]
    return vals.transpose(0, 1, 3, 2).reshape(g * 512, n)


K, T, J, R, V, C, O, U, D, N, E = 512, 1024, 256, 512, 1024, 512, 128, 128, 256, 256, 512


def setup_inputs():
    n = np.random.standard_normal
    idx = np.random.permutation(V)[:R]
    idx2 = np.random.permutation(T)[:J]
    idx3 = np.stack([np.random.permutation(C)[:J] for _ in range(8)])
    idx4 = np.random.permutation(C)[:O]
    idx5 = np.random.permutation(C)[:U]
    idx6 = np.stack([np.random.permutation(E)[:D] for _ in range(8)])
    fk = mx_kscale(K)
    fr = mx_kscale(R)
    tr = np.ones(V)
    tr[idx] = fr
    xtp = pack_weight(n((K, T)) / fk[:, None], "e2m1")
    wtp = pack_weight(n((K, V)) * 1 / np.sqrt(K) * fk[:, None] * tr, "e4m3")
    wbp = pack_weight(n((R, N)) * 1 / np.sqrt(R) / fr[:, None], "e2m1")
    return {
        "xt_words": xtp[0],
        "xt_scales": xtp[1],
        "wt_words": wtp[0],
        "wt_scales": wtp[1],
        "sa": (np.random.uniform(0.5, 1.6, (R, 1))).astype(np.float32),
        "sb": (np.random.uniform(0.5, 1.6, (R, 1))).astype(np.float32),
        "wb_words": wbp[0],
        "wb_scales": wbp[1],
        "offs": striped(idx),
        "offs2": striped(idx2),
        "offs3": striped8(idx3),
        "offs4": striped(idx4),
        "offs5": striped(idx5),
        "offs6": striped8(idx6),
    }


def reference(xt_words, xt_scales, wt_words, wt_scales, sa, sb, wb_words, wb_scales, offs, offs2, offs3, offs4, offs5, offs6):
    idx = unstriped(offs)
    idx2 = unstriped(offs2)
    idx3 = unstriped8(offs3)
    idx4 = unstriped(offs4)
    idx5 = unstriped(offs5)
    idx6 = unstriped8(offs6)
    xtu = unpack_weight(xt_words, xt_scales, "e2m1")
    wtu = unpack_weight(wt_words, wt_scales, "e4m3")
    wbu = unpack_weight(wb_words, wb_scales, "e2m1")
    wtidxg = wtu[:, idx]
    xtidx2g = xtu[:, idx2]
    a = wtidxg.T @ xtidx2g
    pw = np.zeros((R, C))
    pw[np.arange(R)[:, None], idx3[np.arange(R) % 512 // 64]] = a
    h1 = pw[:, idx4] * f64(sa)
    h2 = pw[:, idx5] * f64(sb)
    hid = np.concatenate([h1, h2], axis=1)
    hidq = mxq(hid, 0, "e5m2")
    p = wbu.T @ hidq
    y = np.zeros((N, E))
    y[np.arange(N)[:, None], idx6[np.arange(N) % 128 // 16]] = p
    return y

@@ -1,0 +1,121 @@
+from contextlib import ExitStack
+
+import concourse.mybir as mybir
+
+K, T, J, R, V, C, O, U, D, N, E = 512, 1024, 256, 512, 1024, 512, 128, 128, 256, 256, 512
+FLOPS = 2 * K * R * J + 2 * R * N * D
+
+F32 = mybir.dt.float32
+BF16 = mybir.dt.bfloat16
+I32 = mybir.dt.int32
+U32 = mybir.dt.uint32
+U16 = mybir.dt.uint16
+U8 = mybir.dt.uint8
+E4M3X4 = mybir.dt.float8_e4m3fn_x4
+E5M2X4 = mybir.dt.float8_e5m2_x4
+E2M1X4 = mybir.dt.float4_e2m1fn_x4
+COPY = mybir.ActivationFunctionType.Copy
+
+P = 128
+PACK = 4
+
+
+def tile_list_ownsides_chosen_one_ownpage_kernel(tc, xt_words, xt_scales, wt_words, wt_scales, sa, sb, wb_words, wb_scales,
+                                                    offs, offs2, offs3, offs4, offs5, offs6, out):
+    nc = tc.nc
+    with ExitStack() as ctx:
+        keep = ctx.enter_context(tc.tile_pool(name="keep", bufs=1))
+        psum = ctx.enter_context(tc.psum_pool(name="psum", bufs=1))
+
+        def load_list(src, name):
+            lst = keep.tile([P, src.shape[1]], U16, name=name)
+            nc.sync.dma_start(lst[:], src)
+            return lst
+
+        def scale_tile(width, name):
+            plane = keep.tile([P, width], U8, name=name, align_bytes=64)
+            nc.vector.memset(plane[:].bitcast(I32), 0)
+            return plane
+
+        def load_scales(queue, plane, src):
+            for q in range(4):
+                queue.dma_start(plane[32 * q:32 * q + 4, :].bitcast(I32), src[0, 4 * q:4 * q + 4, :].bitcast(I32))
+
+        wt_s = scale_tile(V, "wt_s")
+        xt_s = scale_tile(T, "xt_s")
+        wb_s = scale_tile(N, "wb_s")
+
+        l1 = load_list(offs, "l1")
+        load_scales(nc.scalar, wt_s, wt_scales)
+        wt_w = keep.tile([P, V], I32, name="wt_w", align_bytes=64)
+        nc.sync.dma_start(wt_w[:], wt_words[0].rearrange("p c r -> p (c r)").bitcast(I32))
+        l2 = load_list(offs2, "l2")
+        xt_w = keep.tile([P, T], U16, name="xt_w", align_bytes=64)
+        nc.sync.dma_start(xt_w[:].bitcast(I32), xt_words[0].bitcast(I32))
+        load_scales(nc.scalar, xt_s, xt_scales)
+        l3 = load_list(offs3, "l3")
+        l4 = load_list(offs4, "l4")
+        l5 = load_list(offs5, "l5")
+        sa_t = keep.tile([P, PACK], F32, name="sa_t")
+        nc.sync.dma_start(sa_t[:], sa.rearrange("(p t) o -> p (t o)", t=PACK))
+        sb_t = keep.tile([P, PACK], F32, name="sb_t")
+        nc.sync.dma_start(sb_t[:], sb.rearrange("(p t) o -> p (t o)", t=PACK))
+        l6 = load_list(offs6, "l6")
+        wb_w = keep.tile([P, 2 * N], U8, name="wb_w", align_bytes=64)
+        nc.sync.dma_start(wb_w[:].bitcast(I32), wb_words[0].bitcast(I32))
+        load_scales(nc.sync, wb_s, wb_scales)
+
+        boards = []
+        for t in range(PACK):
+            board = keep.tile([P, C], F32, name="board%d" % t)
+            nc.vector.memset(board[:], 0.0)
+            boards.append(board)
+        pages = []
+        for u in range(N // P):
+            page = keep.tile([P, E], F32, name="page%d" % u)
+            nc.vector.memset(page[:], 0.0)
+            pages.append(page)
+
+        wg_s = keep.tile([P, PACK, P], U8, name="wg_s", align_bytes=64)
+        nc.vector.tensor_copy(wg_s[:].rearrange("p t m -> p m t"), wt_s[:].indirect(l1[:]))
+        xg_w = keep.tile([P, J], U16, name="xg_w", align_bytes=64)
+        nc.vector.tensor_copy(xg_w[:], xt_w[:].indirect(l2[:]))
+        wg_w = keep.tile([P, PACK, P], U32, name="wg_w", align_bytes=64)
+        nc.vector.tensor_copy(wg_w[:].rearrange("p t m -> p m t"), wt_w[:].bitcast(U32).indirect(l1[:]))
+        xg_s = keep.tile([P, J], U8, name="xg_s", align_bytes=64)
+        nc.vector.tensor_copy(xg_s[:], xt_s[:].indirect(l2[:]))
+
+        for t in range(PACK):
+            acc = psum.tile([P, J], F32, name="acc%d" % t)
+            nc.tensor.matmul_mx(out=acc[:], lhsT=wg_w[:, t, :].bitcast(E4M3X4), lhsT_scale=wg_s[:, t, :],
+                                rhs=xg_w[:].bitcast(E2M1X4), rhs_scale=xg_s[:], start=True, stop=True)
+            a_sb = keep.tile([P, J], F32, name="a_sb%d" % t)
+            nc.vector.tensor_copy(a_sb[:], acc[:])
+            nc.scalar.activation(boards[t][:].indirect(l3[:]), a_sb[:], COPY)
+
+        halves = ((l4, sa_t), (l5, sb_t))
+        p_sb = []
+        for h, (lst, weight) in enumerate(halves):
+            picked = keep.tile([P, PACK, O], BF16, name="picked%d" % h)
+            for t in range(PACK):
+                nc.scalar.activation(picked[:, t, :], boards[t][:].indirect(lst[:]), COPY, scale=weight[:, t:t + 1])
+            woven = keep.tile([P, O, PACK], BF16, name="woven%d" % h, align_bytes=64)
+            nc.vector.tensor_copy(woven[:].rearrange("p (c i) t -> p c t i", i=4), picked[:].rearrange("p t (c i) -> p c t i", i=4))
+            hq_w = keep.tile([P, O], U32, name="hq_w%d" % h, align_bytes=64)
+            hq_s = keep.tile([P, O], U8, name="hq_s%d" % h, align_bytes=64)
+            nc.vector.quantize_mx(out=hq_w[:].bitcast(E5M2X4), scales=hq_s[:], in_=woven[:].rearrange("p c t -> p (c t)"))
+            row = []
+            for u in range(N // P):
+                acc2 = psum.tile([P, O], F32, name="acc2_%d_%d" % (h, u))
+                nc.tensor.matmul_mx(out=acc2[:], lhsT=wb_w[:, 2 * P * u:2 * P * (u + 1)].bitcast(E2M1X4), lhsT_scale=wb_s[:, P * u:P * (u + 1)],
+                                    rhs=hq_w[:].bitcast(E5M2X4), rhs_scale=hq_s[:], start=True, stop=True)
+                res = keep.tile([P, O], F32, name="res%d_%d" % (h, u))
+                nc.vector.tensor_copy(res[:], acc2[:])
+                row.append(res)
+            p_sb.append(row)
+
+        for h in range(2):
+            for u in range(N // P):
+                nc.scalar.activation(pages[u][:].indirect(l6[:, 8 * h:8 * (h + 1)]), p_sb[h][u][:], COPY)
+                if h == 1:
+                    nc.sync.dma_start(out[P * u:P * (u + 1), :], pages[u][:])

@@ -43,16 +43,15 @@ def tile_list_ownsides_chosen_one_ownpage_kernel(tc, xt_words, xt_scales, wt_wor
 
         wt_s = scale_tile(V, "wt_s")
         xt_s = scale_tile(T, "xt_s")
-        wb_s = scale_tile(N, "wb_s")
 
-        l1 = load_list(offs, "l1")
-        load_scales(nc.scalar, wt_s, wt_scales)
-        wt_w = keep.tile([P, V], I32, name="wt_w", align_bytes=64)
-        nc.sync.dma_start(wt_w[:], wt_words[0].rearrange("p c r -> p (c r)").bitcast(I32))
         l2 = load_list(offs2, "l2")
         xt_w = keep.tile([P, T], U16, name="xt_w", align_bytes=64)
         nc.sync.dma_start(xt_w[:].bitcast(I32), xt_words[0].bitcast(I32))
-        load_scales(nc.scalar, xt_s, xt_scales)
+        l1 = load_list(offs, "l1")
+        load_scales(nc.sync, wt_s, wt_scales)
+        wt_w = keep.tile([P, V], I32, name="wt_w", align_bytes=64)
+        nc.sync.dma_start(wt_w[:], wt_words[0].rearrange("p c r -> p (c r)").bitcast(I32))
+        load_scales(nc.sync, xt_s, xt_scales)
         l3 = load_list(offs3, "l3")
         l4 = load_list(offs4, "l4")
         l5 = load_list(offs5, "l5")
@@ -63,54 +62,72 @@ def tile_list_ownsides_chosen_one_ownpage_kernel(tc, xt_words, xt_scales, wt_wor
         l6 = load_list(offs6, "l6")
         wb_w = keep.tile([P, 2 * N], U8, name="wb_w", align_bytes=64)
         nc.sync.dma_start(wb_w[:].bitcast(I32), wb_words[0].bitcast(I32))
-        load_scales(nc.sync, wb_s, wb_scales)
 
         boards = []
         for t in range(PACK):
             board = keep.tile([P, C], F32, name="board%d" % t)
             nc.vector.memset(board[:], 0.0)
             boards.append(board)
+        wb_s = scale_tile(N, "wb_s")
+        load_scales(nc.sync, wb_s, wb_scales)
+
+        HJ = J // 2
+        xg_w = [keep.tile([P, HJ], U16, name="xg_w0", align_bytes=64)]
+        xg_s = [keep.tile([P, HJ], U8, name="xg_s%d" % b, align_bytes=64) for b in range(2)]
+        wg_s = keep.tile([P, PACK, P], U8, name="wg_s", align_bytes=64)
+        wg_w = keep.tile([P, PACK, P], U32, name="wg_w", align_bytes=64)
+        nc.vector.tensor_copy(xg_w[0][:], xt_w[:].indirect(l2[:, 0:8]))
+        nc.vector.tensor_copy(wg_s[:].rearrange("p t m -> p m t"), wt_s[:].indirect(l1[:]))
+        nc.vector.tensor_copy(wg_w[:].rearrange("p t m -> p m t"), wt_w[:].bitcast(U32).indirect(l1[:]))
+        nc.vector.tensor_copy(xg_s[0][:], xt_s[:].indirect(l2[:, 0:8]))
+        nc.vector.tensor_copy(xg_s[1][:], xt_s[:].indirect(l2[:, 8:16]))
+        xg_w.append(keep.tile([P, HJ], U16, name="xg_w1", tag="xt_s", align_bytes=64))
+        nc.vector.tensor_copy(xg_w[1][:], xt_w[:].indirect(l2[:, 8:16]))
+
+        pieces = ((0, 0, HJ), (1, 0, HJ), (0, HJ, J), (1, HJ, J), (2, 0, J), (3, 0, J))
+        for i, (t, j0, j1) in enumerate(pieces):
+            acc = psum.tile([P, j1 - j0], F32, name="acc%d" % i, tag="bank%d" % i)
+            for b in range(j0 // HJ, j1 // HJ):
+                nc.tensor.matmul_mx(out=acc[:, b * HJ - j0:(b + 1) * HJ - j0], lhsT=wg_w[:, t, :].bitcast(E4M3X4), lhsT_scale=wg_s[:, t, :],
+                                    rhs=xg_w[b][:].bitcast(E2M1X4), rhs_scale=xg_s[b][:], start=True, stop=True)
+            a_sb = keep.tile([P, j1 - j0], F32, name="a_sb%d" % i, tag="stage%d" % (i % 4))
+            if i < 2:
+                nc.scalar.copy(a_sb[:], acc[:])
+            else:
+                nc.vector.tensor_copy(a_sb[:], acc[:])
+            nc.scalar.activation(boards[t][:].indirect(l3[:, j0 // 16:j1 // 16]), a_sb[:], COPY)
+
         pages = []
         for u in range(N // P):
-            page = keep.tile([P, E], F32, name="page%d" % u)
+            page = keep.tile([P, E], F32, name="page%d" % u, tag="stage%d" % (u + 2))
             nc.vector.memset(page[:], 0.0)
             pages.append(page)
 
-        wg_s = keep.tile([P, PACK, P], U8, name="wg_s", align_bytes=64)
-        nc.vector.tensor_copy(wg_s[:].rearrange("p t m -> p m t"), wt_s[:].indirect(l1[:]))
-        xg_w = keep.tile([P, J], U16, name="xg_w", align_bytes=64)
-        nc.vector.tensor_copy(xg_w[:], xt_w[:].indirect(l2[:]))
-        wg_w = keep.tile([P, PACK, P], U32, name="wg_w", align_bytes=64)
-        nc.vector.tensor_copy(wg_w[:].rearrange("p t m -> p m t"), wt_w[:].bitcast(U32).indirect(l1[:]))
-        xg_s = keep.tile([P, J], U8, name="xg_s", align_bytes=64)
-        nc.vector.tensor_copy(xg_s[:], xt_s[:].indirect(l2[:]))
-
-        for t in range(PACK):
-            acc = psum.tile([P, J], F32, name="acc%d" % t)
-            nc.tensor.matmul_mx(out=acc[:], lhsT=wg_w[:, t, :].bitcast(E4M3X4), lhsT_scale=wg_s[:, t, :],
-                                rhs=xg_w[:].bitcast(E2M1X4), rhs_scale=xg_s[:], start=True, stop=True)
-            a_sb = keep.tile([P, J], F32, name="a_sb%d" % t)
-            nc.vector.tensor_copy(a_sb[:], acc[:])
-            nc.scalar.activation(boards[t][:].indirect(l3[:]), a_sb[:], COPY)
-
         halves = ((l4, sa_t), (l5, sb_t))
-        p_sb = []
+        picked = []
         for h, (lst, weight) in enumerate(halves):
-            picked = keep.tile([P, PACK, O], BF16, name="picked%d" % h)
+            pk = keep.tile([P, PACK, O], BF16, name="picked%d" % h, tag=("picked0", "stage1")[h])
             for t in range(PACK):
-                nc.scalar.activation(picked[:, t, :], boards[t][:].indirect(lst[:]), COPY, scale=weight[:, t:t + 1])
-            woven = keep.tile([P, O, PACK], BF16, name="woven%d" % h, align_bytes=64)
-            nc.vector.tensor_copy(woven[:].rearrange("p (c i) t -> p c t i", i=4), picked[:].rearrange("p t (c i) -> p c t i", i=4))
+                nc.scalar.activation(pk[:, t, :], boards[t][:].indirect(lst[:]), COPY, scale=weight[:, t:t + 1])
+            picked.append(pk)
+        p_sb = []
+        for h in range(2):
+            woven = keep.tile([P, O, PACK], BF16, name="woven%d" % h, tag="woven", align_bytes=64)
+            for t0 in (0, 2):
+                nc.vector.tensor_copy(woven[:, :, t0:t0 + 2], picked[h][:, t0:t0 + 2, :].rearrange("p t c -> p c t"))
             hq_w = keep.tile([P, O], U32, name="hq_w%d" % h, align_bytes=64)
             hq_s = keep.tile([P, O], U8, name="hq_s%d" % h, align_bytes=64)
             nc.vector.quantize_mx(out=hq_w[:].bitcast(E5M2X4), scales=hq_s[:], in_=woven[:].rearrange("p c t -> p (c t)"))
             row = []
             for u in range(N // P):
-                acc2 = psum.tile([P, O], F32, name="acc2_%d_%d" % (h, u))
+                acc2 = psum.tile([P, O], F32, name="acc2_%d_%d" % (h, u), tag="bank%d" % (2 * h + u))
                 nc.tensor.matmul_mx(out=acc2[:], lhsT=wb_w[:, 2 * P * u:2 * P * (u + 1)].bitcast(E2M1X4), lhsT_scale=wb_s[:, P * u:P * (u + 1)],
                                     rhs=hq_w[:].bitcast(E5M2X4), rhs_scale=hq_s[:], start=True, stop=True)
                 res = keep.tile([P, O], F32, name="res%d_%d" % (h, u))
-                nc.vector.tensor_copy(res[:], acc2[:])
+                if h == 0 and u == 0:
+                    nc.scalar.copy(res[:], acc2[:])
+                else:
+                    nc.vector.tensor_copy(res[:], acc2[:])
                 row.append(res)
             p_sb.append(row)
 

@@ -64,7 +64,7 @@ def tile_list_ownsides_chosen_one_ownpage_kernel(tc, xt_words, xt_scales, wt_wor
         nc.sync.dma_start(wb_w[:].bitcast(I32), wb_words[0].bitcast(I32))
 
         boards = []
-        for t in range(PACK):
+        for t in range(2):
             board = keep.tile([P, C], F32, name="board%d" % t)
             nc.vector.memset(board[:], 0.0)
             boards.append(board)
@@ -86,6 +86,10 @@ def tile_list_ownsides_chosen_one_ownpage_kernel(tc, xt_words, xt_scales, wt_wor
 
         pieces = ((0, 0, HJ), (1, 0, HJ), (0, HJ, J), (1, HJ, J), (2, 0, J), (3, 0, J))
         for i, (t, j0, j1) in enumerate(pieces):
+            if t == len(boards):
+                board = keep.tile([P, C], F32, name="board%d" % t, tag=("xt_w", "xt_s")[t - 2], align_bytes=64)
+                nc.vector.memset(board[:], 0.0)
+                boards.append(board)
             acc = psum.tile([P, j1 - j0], F32, name="acc%d" % i, tag="bank%d" % i)
             for b in range(j0 // HJ, j1 // HJ):
                 nc.tensor.matmul_mx(out=acc[:, b * HJ - j0:(b + 1) * HJ - j0], lhsT=wg_w[:, t, :].bitcast(E4M3X4), lhsT_scale=wg_s[:, t, :],

from contextlib import ExitStack

import concourse.mybir as mybir

K, T, J, R, V, C, O, U, D, N, E = 512, 1024, 256, 512, 1024, 512, 128, 128, 256, 256, 512
FLOPS = 2 * K * R * J + 2 * R * N * D

F32 = mybir.dt.float32
BF16 = mybir.dt.bfloat16
I32 = mybir.dt.int32
U32 = mybir.dt.uint32
U16 = mybir.dt.uint16
U8 = mybir.dt.uint8
E4M3X4 = mybir.dt.float8_e4m3fn_x4
E5M2X4 = mybir.dt.float8_e5m2_x4
E2M1X4 = mybir.dt.float4_e2m1fn_x4
COPY = mybir.ActivationFunctionType.Copy

P = 128
PACK = 4


def tile_list_ownsides_chosen_one_ownpage_kernel(tc, xt_words, xt_scales, wt_words, wt_scales, sa, sb, wb_words, wb_scales,
                                                    offs, offs2, offs3, offs4, offs5, offs6, out):
    nc = tc.nc
    with ExitStack() as ctx:
        keep = ctx.enter_context(tc.tile_pool(name="keep", bufs=1))
        psum = ctx.enter_context(tc.psum_pool(name="psum", bufs=1))

        def load_list(src, name):
            lst = keep.tile([P, src.shape[1]], U16, name=name)
            nc.sync.dma_start(lst[:], src)
            return lst

        def scale_tile(width, name):
            plane = keep.tile([P, width], U8, name=name, align_bytes=64)
            nc.vector.memset(plane[:].bitcast(I32), 0)
            return plane

        def load_scales(queue, plane, src):
            for q in range(4):
                queue.dma_start(plane[32 * q:32 * q + 4, :].bitcast(I32), src[0, 4 * q:4 * q + 4, :].bitcast(I32))

        wt_s = scale_tile(V, "wt_s")
        xt_s = scale_tile(T, "xt_s")

        l2 = load_list(offs2, "l2")
        xt_w = keep.tile([P, T], U16, name="xt_w", align_bytes=64)
        nc.sync.dma_start(xt_w[:].bitcast(I32), xt_words[0].bitcast(I32))
        l1 = load_list(offs, "l1")
        load_scales(nc.sync, wt_s, wt_scales)
        wt_w = keep.tile([P, V], I32, name="wt_w", align_bytes=64)
        nc.sync.dma_start(wt_w[:], wt_words[0].rearrange("p c r -> p (c r)").bitcast(I32))
        load_scales(nc.sync, xt_s, xt_scales)
        l3 = load_list(offs3, "l3")
        l4 = load_list(offs4, "l4")
        l5 = load_list(offs5, "l5")
        sa_t = keep.tile([P, PACK], F32, name="sa_t")
        nc.sync.dma_start(sa_t[:], sa.rearrange("(p t) o -> p (t o)", t=PACK))
        sb_t = keep.tile([P, PACK], F32, name="sb_t")
        nc.sync.dma_start(sb_t[:], sb.rearrange("(p t) o -> p (t o)", t=PACK))
        l6 = load_list(offs6, "l6")
        wb_w = keep.tile([P, 2 * N], U8, name="wb_w", align_bytes=64)
        nc.sync.dma_start(wb_w[:].bitcast(I32), wb_words[0].bitcast(I32))

        boards = []
        for t in range(2):
            board = keep.tile([P, C], F32, name="board%d" % t)
            nc.vector.memset(board[:], 0.0)
            boards.append(board)
        wb_s = scale_tile(N, "wb_s")
        load_scales(nc.sync, wb_s, wb_scales)

        HJ = J // 2
        xg_w = [keep.tile([P, HJ], U16, name="xg_w0", align_bytes=64)]
        xg_s = [keep.tile([P, HJ], U8, name="xg_s%d" % b, align_bytes=64) for b in range(2)]
        wg_s = keep.tile([P, PACK, P], U8, name="wg_s", align_bytes=64)
        wg_w = keep.tile([P, PACK, P], U32, name="wg_w", align_bytes=64)
        nc.vector.tensor_copy(xg_w[0][:], xt_w[:].indirect(l2[:, 0:8]))
        nc.vector.tensor_copy(wg_s[:].rearrange("p t m -> p m t"), wt_s[:].indirect(l1[:]))
        nc.vector.tensor_copy(wg_w[:].rearrange("p t m -> p m t"), wt_w[:].bitcast(U32).indirect(l1[:]))
        nc.vector.tensor_copy(xg_s[0][:], xt_s[:].indirect(l2[:, 0:8]))
        nc.vector.tensor_copy(xg_s[1][:], xt_s[:].indirect(l2[:, 8:16]))
        xg_w.append(keep.tile([P, HJ], U16, name="xg_w1", tag="xt_s", align_bytes=64))
        nc.vector.tensor_copy(xg_w[1][:], xt_w[:].indirect(l2[:, 8:16]))

        pieces = ((0, 0, HJ), (1, 0, HJ), (0, HJ, J), (1, HJ, J), (2, 0, J), (3, 0, J))
        for i, (t, j0, j1) in enumerate(pieces):
            if t == len(boards):
                board = keep.tile([P, C], F32, name="board%d" % t, tag=("xt_w", "xt_s")[t - 2], align_bytes=64)
                nc.vector.memset(board[:], 0.0)
                boards.append(board)
            acc = psum.tile([P, j1 - j0], F32, name="acc%d" % i, tag="bank%d" % i)
            for b in range(j0 // HJ, j1 // HJ):
                nc.tensor.matmul_mx(out=acc[:, b * HJ - j0:(b + 1) * HJ - j0], lhsT=wg_w[:, t, :].bitcast(E4M3X4), lhsT_scale=wg_s[:, t, :],
                                    rhs=xg_w[b][:].bitcast(E2M1X4), rhs_scale=xg_s[b][:], start=True, stop=True)
            a_sb = keep.tile([P, j1 - j0], F32, name="a_sb%d" % i, tag="stage%d" % (i % 4))
            if i < 2:
                nc.scalar.copy(a_sb[:], acc[:])
            else:
                nc.vector.tensor_copy(a_sb[:], acc[:])
            nc.scalar.activation(boards[t][:].indirect(l3[:, j0 // 16:j1 // 16]), a_sb[:], COPY)

        pages = []
        for u in range(N // P):
            page = keep.tile([P, E], F32, name="page%d" % u, tag="stage%d" % (u + 2))
            nc.vector.memset(page[:], 0.0)
            pages.append(page)

        halves = ((l4, sa_t), (l5, sb_t))
        picked = []
        for h, (lst, weight) in enumerate(halves):
            pk = keep.tile([P, PACK, O], BF16, name="picked%d" % h, tag=("picked0", "stage1")[h])
            for t in range(PACK):
                nc.scalar.activation(pk[:, t, :], boards[t][:].indirect(lst[:]), COPY, scale=weight[:, t:t + 1])
            picked.append(pk)
        p_sb = []
        for h in range(2):
            woven = keep.tile([P, O, PACK], BF16, name="woven%d" % h, tag="woven", align_bytes=64)
            for t0 in (0, 2):
                nc.vector.tensor_copy(woven[:, :, t0:t0 + 2], picked[h][:, t0:t0 + 2, :].rearrange("p t c -> p c t"))
            hq_w = keep.tile([P, O], U32, name="hq_w%d" % h, align_bytes=64)
            hq_s = keep.tile([P, O], U8, name="hq_s%d" % h, align_bytes=64)
            nc.vector.quantize_mx(out=hq_w[:].bitcast(E5M2X4), scales=hq_s[:], in_=woven[:].rearrange("p c t -> p (c t)"))
            row = []
            for u in range(N // P):
                acc2 = psum.tile([P, O], F32, name="acc2_%d_%d" % (h, u), tag="bank%d" % (2 * h + u))
                nc.tensor.matmul_mx(out=acc2[:], lhsT=wb_w[:, 2 * P * u:2 * P * (u + 1)].bitcast(E2M1X4), lhsT_scale=wb_s[:, P * u:P * (u + 1)],
                                    rhs=hq_w[:].bitcast(E5M2X4), rhs_scale=hq_s[:], start=True, stop=True)
                res = keep.tile([P, O], F32, name="res%d_%d" % (h, u))
                if h == 0 and u == 0:
                    nc.scalar.copy(res[:], acc2[:])
                else:
                    nc.vector.tensor_copy(res[:], acc2[:])
                row.append(res)
            p_sb.append(row)

        for h in range(2):
            for u in range(N // P):
                nc.scalar.activation(pages[u][:].indirect(l6[:, 8 * h:8 * (h + 1)]), p_sb[h][u][:], COPY)
                if h == 1:
                    nc.sync.dma_start(out[P * u:P * (u + 1), :], pages[u][:])
